import numpy as np
import ml_dtypes


def mxq(x, axis, fmt="e4m3"):
    dtype, down = {"e4m3": (ml_dtypes.float8_e4m3fn, 7), "e5m2": (ml_dtypes.float8_e5m2, 14)}[fmt]
    v = np.moveaxis(np.asarray(x, np.float32).astype(ml_dtypes.bfloat16).astype(np.float64), axis, -1)
    blocks = v.reshape(v.shape[:-1] + (-1, 32))
    amax = np.abs(blocks).max(-1, keepdims=True)
    byte = np.maximum(np.where(amax > 0, np.frexp(amax)[1] - 1 + 127, 0) - down, 1)
    scale = np.exp2(byte - 127.0)
    codes = (blocks / scale).astype(np.float32).astype(dtype).astype(np.float64)
    return np.moveaxis((codes * scale).reshape(v.shape), -1, axis)


WIDE = False


def mx_kscale(k):
    if not WIDE:
        return np.ones(k)
    levels = np.array([10, -10, 5, -5, 0])
    if k % 512:
        return np.exp2(np.random.permutation(np.resize(levels, k // 32))).repeat(32)
    a = np.empty((k // 512, 16))
    for p in range(k // 512):
        a[p, :8] = np.random.permutation(np.resize(levels, 8))
        for g in range(8):
            far = levels[np.abs(levels - a[p, g]) >= 10]
            a[p, g + 8] = far[np.random.randint(len(far))]
    return np.exp2(a.ravel()).repeat(32)


def f64(x):
    return np.asarray(x).astype(np.float64)


def striped(idx):
    return np.tile(np.asarray(idx).reshape(-1, 16).T, (8, 1)).astype(np.uint16)


def unstriped(offs):
    return offs[:16].T.reshape(-1).astype(np.int64)


def striped8(idx):
    return np.asarray(idx).reshape(8, -1, 16).transpose(0, 2, 1).reshape(128, -1).astype(np.uint16)


def unstriped8(offs):
    return offs.reshape(8, 16, -1).transpose(0, 2, 1).reshape(8, -1).astype(np.int64)


def pick8(x, idx, run):
    r = np.arange(len(x))
    return x[r[:, None], idx[r % (8 * run) // run]]


E2M1 = np.array([0.0, 0.5, 1.0, 1.5, 2.0, 3.0, 4.0, 6.0, -0.0, -0.5, -1.0, -1.5, -2.0, -3.0, -4.0, -6.0])


def pack_weight(w, fmt):
    k, n = w.shape
    w = f64(np.asarray(w, np.float32).astype(ml_dtypes.bfloat16)).reshape(k // 32, 32, n)
    amax = np.abs(w).max(1)
    if fmt == "e4m3":
        byte = np.frexp(amax)[1] - 1 + 127 - 7
    else:
        mant, ex = np.frexp(amax / 6.0)
        byte = np.where(mant > 0.5, ex, ex - 1) + 127
    byte = np.clip(np.where(amax > 0, byte, 1), 1, 254)
    scaled = (w * np.exp2(127.0 - byte)[:, None, :]).reshape(k, n).astype(np.float32)
    by_word = np.ascontiguousarray(scaled.reshape(k // 512, 128, 4, n).transpose(0, 1, 3, 2))
    if fmt == "e4m3":
        words = by_word.astype(ml_dtypes.float8_e4m3fn).view(np.uint8)
    else:
        c = by_word.astype(ml_dtypes.float4_e2m1fn).view(np.uint8) & 0xF
        words = (c[..., 0::2] | (c[..., 1::2] << 4)).reshape(k // 512, 128, 2 * n)
    return np.ascontiguousarray(words), np.ascontiguousarray(byte.astype(np.uint8).reshape(k // 512, 16, n))


def unpack_weight(words, scales, fmt):
    g, _, n = scales.shape
    words = np.ascontiguousarray(words).reshape(g, 128, n, -1)
    if fmt == "e4m3":
        vals = words.view(ml_dtypes.float8_e4m3fn).astype(np.float64)
    else:
        nib = np.empty((g, 128, n, 4), np.uint8)
        nib[..., 0::2] = words & 0xF
        nib[..., 1::2] = words >> 4
        vals = E2M1[nib]
    vals = vals * np.repeat(np.exp2(scales.astype(np.float64) - 127.0), 8, axis=1)[..., None]
    return vals.transpose(0, 1, 3, 2).reshape(g * 512, n)


def sgn(shape):
    return np.random.uniform(0.5, 2.0, shape) * np.where(np.random.standard_normal(shape) < 0, -1.0, 1.0)


K, J, R, T, U, O, D, N, S, Z, E, G = 512, 512, 512, 1024, 1024, 256, 1024, 256, 512, 1024, 128, 512


def setup_inputs():
    n = np.random.standard_normal
    idx = np.random.permutation(T)[:J]
    idx2 = np.stack([np.random.permutation(U)[:J] for _ in range(8)])
    idx3 = np.stack([np.random.permutation(J)[:O] for _ in range(8)])
    idx4 = np.stack([np.random.permutation(D)[:O] for _ in range(8)])
    idx5 = np.random.permutation(Z)[:O]
    idx6 = np.stack([np.random.permutation(O)[:E] for _ in range(8)])
    idx7 = np.stack([np.random.permutation(G)[:E] for _ in range(8)])
    fk = mx_kscale(K)
    fr = mx_kscale(R)
    fs = mx_kscale(S)
    wp = pack_weight(n((K, R)) * 1 / np.sqrt(K) / fk[:, None] * fr, "e2m1")
    wbp = pack_weight(n((R, N)) * 1 / np.sqrt(R) / fr[:, None], "e4m3")
    xrp = pack_weight(n((S, Z)) / fs[:, None], "e4m3")
    wsp = pack_weight(n((S, N)) * 1 / np.sqrt(S) * fs[:, None], "e2m1")
    return {
        "ta": (np.random.randint(-7, 8, (K, T)).astype(np.float64)).astype(np.float32),
        "tb": (np.random.randint(-7, 8, (K, U)).astype(np.float64)).astype(np.float32),
        "ga": ((np.random.randint(10, 25, (K, 1)) / 64.0) * fk[:, None]).astype(np.float32),
        "gb": ((np.random.randint(4, 13, (K, 1)) / 64.0) * fk[:, None]).astype(np.float32),
        "w_words": wp[0],
        "w_scales": wp[1],
        "tl": (np.random.randint(-7, 8, (R, D)).astype(np.float64)).astype(np.float32),
        "sa": (np.random.uniform(0.5, 1.6, (R, 1))).astype(np.float32),
        "sl": ((np.random.randint(6, 19, (R, 1)) / 64.0) * fr[:, None]).astype(np.float32),
        "wb_words": wbp[0],
        "wb_scales": wbp[1],
        "xr_words": xrp[0],
        "xr_scales": xrp[1],
        "ws_words": wsp[0],
        "ws_scales": wsp[1],
        "so": (sgn((N, 1))).astype(np.float32),
        "offs": striped(idx),
        "offs2": striped8(idx2),
        "offs3": striped8(idx3),
        "offs4": striped8(idx4),
        "offs5": striped(idx5),
        "offs6": striped8(idx6),
        "offs7": striped8(idx7),
    }


def reference(ta, tb, ga, gb, w_words, w_scales, tl, sa, sl, wb_words, wb_scales, xr_words, xr_scales, ws_words, ws_scales, so, offs, offs2, offs3, offs4, offs5, offs6, offs7):
    idx = unstriped(offs)
    idx2 = unstriped8(offs2)
    idx3 = unstriped8(offs3)
    idx4 = unstriped8(offs4)
    idx5 = unstriped(offs5)
    idx6 = unstriped8(offs6)
    idx7 = unstriped8(offs7)
    wu = unpack_weight(w_words, w_scales, "e2m1")
    wbu = unpack_weight(wb_words, wb_scales, "e4m3")
    xru = unpack_weight(xr_words, xr_scales, "e4m3")
    wsu = unpack_weight(ws_words, ws_scales, "e2m1")
    xc = f64(ta)[:, idx] * f64(ga) + pick8(f64(tb), idx2, 64) * f64(gb)
    xcq = mxq(xc, 0, "e4m3")
    a = wu.T @ xcq
    hid = np.maximum(pick8(a, idx3, 64) * f64(sa), pick8(f64(tl), idx4, 64) * f64(sl))
    hidq = mxq(hid, 0, "e4m3")
    xridx5g = xru[:, idx5]
    p = wbu.T @ hidq + wsu.T @ xridx5g
    m0 = pick8(p, idx6, 16) * f64(so)
    y = np.zeros((N, G))
    y[np.arange(N)[:, None], idx7[np.arange(N) % 128 // 16]] = m0
    return y

@@ -1,0 +1,226 @@
+from contextlib import ExitStack
+
+import concourse.mybir as mybir
+
+K, J, R, T, O, N, Z, E, G = 512, 512, 512, 1024, 256, 256, 1024, 128, 512
+FLOPS = 2 * K * R * J + 2 * R * N * O + 2 * 512 * N * O
+
+F32 = mybir.dt.float32
+BF16 = mybir.dt.bfloat16
+I32 = mybir.dt.int32
+U32 = mybir.dt.uint32
+U16 = mybir.dt.uint16
+U8 = mybir.dt.uint8
+FP8X4 = mybir.dt.float8_e4m3fn_x4
+FP4X4 = mybir.dt.float4_e2m1fn_x4
+COPY = mybir.ActivationFunctionType.Copy
+ADD = mybir.AluOpType.add
+MAX = mybir.AluOpType.max
+
+P = 128
+PACK = 4
+HALVES = 2
+
+
+def tile_picked_basedetail_plain_one_codedlevel_reminder_posted_kernel(
+    tc, ta, tb, ga, gb, w_words, w_scales, tl, sa, sl, wb_words, wb_scales, xr_words, xr_scales,
+    ws_words, ws_scales, so, offs, offs2, offs3, offs4, offs5, offs6, offs7, out,
+):
+    nc = tc.nc
+    JH = J // HALVES
+    OH = O // HALVES
+    with ExitStack() as ctx:
+        sb = ctx.enter_context(tc.tile_pool(name="sb", bufs=1))
+        ps = ctx.enter_context(tc.psum_pool(name="ps", bufs=1))
+
+        def load_list(src, name):
+            dst = sb.tile(list(src.shape), U16, name=name)
+            nc.sync.dma_start(dst[:], src)
+            return dst
+
+        def load_rows(table, t, name):
+            dst = sb.tile([P, table.shape[1]], F32, name=name)
+            nc.sync.dma_start(out=dst[:], in_=table.rearrange("(p t) c -> p t c", t=PACK)[:, t, :])
+            return dst
+
+        def load_factor(engine, vec, name):
+            dst = sb.tile([P, PACK], F32, name=name)
+            engine.dma_start(out=dst[:], in_=vec.rearrange("(p t) o -> p (t o)", t=PACK))
+            return dst
+
+        def load_words(src, name):
+            dst = sb.tile([P, src.shape[1]], U8, name=name, align_bytes=64)
+            nc.sync.dma_start(out=dst[:].bitcast(I32), in_=src.bitcast(I32))
+            return dst
+
+        def load_scales(src, name):
+            width = src.shape[2]
+            stage = sb.tile([4, 4, width // 4], I32, name=name + "_stage")
+            nc.sync.dma_start(out=stage[:], in_=src[0].bitcast(I32).rearrange("(q i) c -> i q c", i=4))
+            plane = sb.tile([P, width], U8, name=name, align_bytes=64)
+            nc.vector.memset(plane[:].bitcast(I32), 0)
+            for q in range(4):
+                nc.vector.tensor_copy(out=plane[32 * q : 32 * q + 4, :].bitcast(I32), in_=stage[:, q, :])
+            return plane
+
+        def cols16(lst, lo, hi):
+            return lst[:, lo // 16 : hi // 16]
+
+        def scaled_gather(dst, window, offsets, factor):
+            nc.scalar.activation(out=dst, in_=window[:].indirect(offsets), func=COPY, scale=factor)
+
+        def combine_interleaved(dst, left, right, op):
+            nc.vector.tensor_tensor(
+                out=dst[:].rearrange("p (c i t) -> p c t i", i=4, t=PACK),
+                in0=left.rearrange("p t (c i) -> p c t i", i=4),
+                in1=right.rearrange("p t (c i) -> p c t i", i=4),
+                op=op,
+            )
+
+        ga_sb = load_factor(nc.scalar, ga, "ga_sb")
+        gb_sb = load_factor(nc.scalar, gb, "gb_sb")
+        l1 = load_list(offs, "l1")
+        ta_sb = [load_rows(ta, 0, "ta0")]
+        l2 = load_list(offs2, "l2")
+        tb_sb = [load_rows(tb, 0, "tb0")]
+        ta_sb.append(load_rows(ta, 1, "ta1"))
+        tb_sb.append(load_rows(tb, 1, "tb1"))
+        ta_sb.append(load_rows(ta, 2, "ta2"))
+        w_sc_raw = load_scales(w_scales, "w_sc_raw")
+        tb_sb.append(load_rows(tb, 2, "tb2"))
+        sl_sb = load_factor(nc.sync, sl, "sl_sb")
+        ta_sb.append(load_rows(ta, 3, "ta3"))
+        l4 = load_list(offs4, "l4")
+        tb_sb.append(load_rows(tb, 3, "tb3"))
+        w_raw = load_words(w_words[0], "w_raw")
+        tl_sb = [load_rows(tl, 0, "tl0")]
+        l3 = load_list(offs3, "l3")
+        sa_sb = load_factor(nc.sync, sa, "sa_sb")
+        tl_sb.append(load_rows(tl, 1, "tl1"))
+        l5 = load_list(offs5, "l5")
+        xr_sc = load_scales(xr_scales, "xr_sc")
+        tl_sb.append(load_rows(tl, 2, "tl2"))
+        ws_sc = load_scales(ws_scales, "ws_sc")
+        wb_sc = load_scales(wb_scales, "wb_sc")
+        tl_sb.append(load_rows(tl, 3, "tl3"))
+        xr_sb = load_words(xr_words[0].rearrange("p n t -> p (n t)"), "xr_sb")
+        ws_sb = load_words(ws_words[0], "ws_sb")
+        wb_sb = load_words(wb_words[0].rearrange("p n t -> p (n t)"), "wb_sb")
+        so_sb = sb.tile([P, N // P], F32, name="so_sb")
+        with nc.allow_non_contiguous_dma(reason="one factor a partition"):
+            nc.sync.dma_start(out=so_sb[:], in_=so.rearrange("(b p) o -> p (b o)", p=P))
+        l6 = load_list(offs6, "l6")
+        l7 = load_list(offs7, "l7")
+
+        page = [sb.tile([P, G], F32, name="page%d" % b) for b in range(N // P)]
+        for b in range(N // P):
+            nc.vector.memset(page[b][:], 0.0)
+
+        w_sc = sb.tile([P, R], U8, name="w_sc", align_bytes=64)
+        nc.vector.tensor_copy(
+            out=w_sc[:].rearrange("p (t m) -> p t m", t=PACK),
+            in_=w_sc_raw[:].rearrange("p (m t) -> p t m", t=PACK),
+        )
+        w_sb = sb.tile([P, 2 * R], U8, name="w_sb", align_bytes=64)
+        nc.vector.tensor_copy(
+            out=w_sb[:].rearrange("p (t m y) -> p t m y", t=PACK, y=2),
+            in_=w_raw[:].rearrange("p (m t y) -> p t m y", t=PACK, y=2),
+        )
+
+        base = sb.tile([P, PACK, J], F32, name="base")
+        detail = sb.tile([P, PACK, J], F32, name="detail")
+        for t in range(PACK - 1):
+            scaled_gather(base[:, t, :], ta_sb[t], l1[:], ga_sb[:, t : t + 1])
+            scaled_gather(detail[:, t, :], tb_sb[t], l2[:], gb_sb[:, t : t + 1])
+        t = PACK - 1
+        scaled_gather(base[:, t, :], ta_sb[t], l1[:], ga_sb[:, t : t + 1])
+        a_sb = [sb.tile([P, J], F32, name="a%d" % t) for t in range(PACK)]
+        for h in range(HALVES):
+            lo, hi = h * JH, (h + 1) * JH
+            scaled_gather(detail[:, PACK - 1, lo:hi], tb_sb[PACK - 1], cols16(l2, lo, hi), gb_sb[:, PACK - 1 : PACK])
+        banks1 = []
+        for h in range(HALVES):
+            lo, hi = h * JH, (h + 1) * JH
+            xb = sb.tile([P, PACK * JH], BF16, name="xb%d" % h, align_bytes=64)
+            combine_interleaved(xb, base[:, :, lo:hi], detail[:, :, lo:hi], ADD)
+            xq = sb.tile([P, JH], U32, name="xq%d" % h, align_bytes=64)
+            xs = sb.tile([P, JH], U8, name="xs%d" % h, align_bytes=64)
+            nc.vector.quantize_mx(out=xq[:].bitcast(FP8X4), scales=xs[:], in_=xb[:])
+            pair = []
+            for u in range(2):
+                bank = ps.tile([P, 2, JH], F32, name="a_ps%d%d" % (h, u))
+                for v in range(2):
+                    t = 2 * u + v
+                    nc.tensor.matmul_mx(
+                        out=bank[:, v, :],
+                        lhsT=w_sb[:, 2 * P * t : 2 * P * (t + 1)].bitcast(FP4X4),
+                        lhsT_scale=w_sc[:, P * t : P * (t + 1)],
+                        rhs=xq[:].bitcast(FP8X4),
+                        rhs_scale=xs[:],
+                        start=True,
+                        stop=True,
+                    )
+                pair.append(bank)
+            banks1.append(pair)
+
+        level = sb.tile([P, PACK, O], F32, name="level")
+        for t in range(2):
+            scaled_gather(level[:, t, :], tl_sb[t], l4[:], sl_sb[:, t : t + 1])
+        for t in range(PACK):
+            nc.scalar.copy(out=a_sb[t][:, 0:JH], in_=banks1[0][t // 2][:, t % 2, :])
+        for t in range(PACK):
+            nc.vector.tensor_copy(out=a_sb[t][:, JH:J], in_=banks1[1][t // 2][:, t % 2, :])
+        scaled_gather(level[:, 2, :], tl_sb[2], l4[:], sl_sb[:, 2:3])
+
+        picked = sb.tile([P, PACK, O], F32, name="picked")
+        for t in range(PACK):
+            scaled_gather(picked[:, t, 0:OH], a_sb[t], cols16(l3, 0, OH), sa_sb[:, t : t + 1])
+        scaled_gather(level[:, 3, :], tl_sb[3], l4[:], sl_sb[:, 3:4])
+        for t in range(PACK):
+            scaled_gather(picked[:, t, OH:O], a_sb[t], cols16(l3, OH, O), sa_sb[:, t : t + 1])
+
+        xr_gs = sb.tile([P, O], U8, name="xr_gs", align_bytes=64)
+        nc.vector.tensor_copy(out=xr_gs[:], in_=xr_sc[:].indirect(l5[:]))
+        xr_g = sb.tile([P, O], U32, name="xr_g", align_bytes=64)
+
+        p_sb = [sb.tile([P, O], F32, name="p%d" % b) for b in range(N // P)]
+        for h in range(HALVES):
+            lo, hi = h * OH, (h + 1) * OH
+            hb = sb.tile([P, PACK * OH], BF16, name="hb%d" % h, align_bytes=64)
+            combine_interleaved(hb, picked[:, :, lo:hi], level[:, :, lo:hi], MAX)
+            hq = sb.tile([P, OH], U32, name="hq%d" % h, align_bytes=64)
+            hs = sb.tile([P, OH], U8, name="hs%d" % h, align_bytes=64)
+            nc.vector.quantize_mx(out=hq[:].bitcast(FP8X4), scales=hs[:], in_=hb[:])
+            if h == 0:
+                nc.vector.tensor_copy(out=xr_g[:], in_=xr_sb[:].bitcast(U32).indirect(l5[:]))
+            banks2 = []
+            for b in range(N // P):
+                bank = ps.tile([P, OH], F32, name="p_ps%d%d" % (h, b))
+                nc.tensor.matmul_mx(
+                    out=bank[:],
+                    lhsT=ws_sb[:, 2 * P * b : 2 * P * (b + 1)].bitcast(FP4X4),
+                    lhsT_scale=ws_sc[:, P * b : P * (b + 1)],
+                    rhs=xr_g[:, lo:hi].bitcast(FP8X4),
+                    rhs_scale=xr_gs[:, lo:hi],
+                    start=True,
+                    stop=False,
+                )
+                banks2.append(bank)
+            for b in range(N // P):
+                nc.tensor.matmul_mx(
+                    out=banks2[b][:],
+                    lhsT=wb_sb[:, 4 * P * b : 4 * P * (b + 1)].bitcast(FP8X4),
+                    lhsT_scale=wb_sc[:, P * b : P * (b + 1)],
+                    rhs=hq[:].bitcast(FP8X4),
+                    rhs_scale=hs[:],
+                    start=False,
+                    stop=True,
+                )
+            for b in range(N // P):
+                nc.vector.tensor_copy(out=p_sb[b][:, lo:hi], in_=banks2[b][:])
+
+        for b in range(N // P):
+            ends = sb.tile([P, E], F32, name="ends%d" % b)
+            scaled_gather(ends[:], p_sb[b], l6[:], so_sb[:, b : b + 1])
+            nc.vector.tensor_copy(out=page[b][:].indirect(l7[:]), in_=ends[:])
+            nc.sync.dma_start(out=out[P * b : P * (b + 1), :], in_=page[b][:])

@@ -39,7 +39,7 @@ def tile_picked_basedetail_plain_one_codedlevel_reminder_posted_kernel(
             return dst
 
         def load_rows(table, t, name):
-            dst = sb.tile([P, table.shape[1]], F32, name=name)
+            dst = sb.tile([P, table.shape[1]], F32, name=name, tag=name)
             nc.sync.dma_start(out=dst[:], in_=table.rearrange("(p t) c -> p t c", t=PACK)[:, t, :])
             return dst
 
@@ -49,7 +49,7 @@ def tile_picked_basedetail_plain_one_codedlevel_reminder_posted_kernel(
             return dst
 
         def load_words(src, name):
-            dst = sb.tile([P, src.shape[1]], U8, name=name, align_bytes=64)
+            dst = sb.tile([P, src.shape[1]], U8, name=name, tag=name, align_bytes=64)
             nc.sync.dma_start(out=dst[:].bitcast(I32), in_=src.bitcast(I32))
             return dst
 
@@ -69,39 +69,46 @@ def tile_picked_basedetail_plain_one_codedlevel_reminder_posted_kernel(
         def scaled_gather(dst, window, offsets, factor):
             nc.scalar.activation(out=dst, in_=window[:].indirect(offsets), func=COPY, scale=factor)
 
-        def combine_interleaved(dst, left, right, op):
+        def combine_pair(dst, left, right, op, lo, hi, t0):
             nc.vector.tensor_tensor(
-                out=dst[:].rearrange("p (c i t) -> p c t i", i=4, t=PACK),
-                in0=left.rearrange("p t (c i) -> p c t i", i=4),
-                in1=right.rearrange("p t (c i) -> p c t i", i=4),
+                out=dst[:, PACK * lo : PACK * hi].rearrange("p (c i t) -> p c t i", i=2, t=PACK)[:, :, t0 : t0 + 2, :],
+                in0=left[:, :, lo:hi].rearrange("p t (c i) -> p c t i", i=2),
+                in1=right[:, :, lo:hi].rearrange("p t (c i) -> p c t i", i=2),
                 op=op,
             )
 
+        warm = sb.tile([P, 2], F32, name="warm")
+        nc.gpsimd.memset(warm[:, 0:1], 0.0)
+        nc.scalar.activation(out=warm[:, 1:2], in_=warm[:, 0:1], func=COPY)
         ga_sb = load_factor(nc.scalar, ga, "ga_sb")
         gb_sb = load_factor(nc.scalar, gb, "gb_sb")
-        l1 = load_list(offs, "l1")
         ta_sb = [load_rows(ta, 0, "ta0")]
+        l1 = load_list(offs, "l1")
         l2 = load_list(offs2, "l2")
         tb_sb = [load_rows(tb, 0, "tb0")]
         ta_sb.append(load_rows(ta, 1, "ta1"))
-        tb_sb.append(load_rows(tb, 1, "tb1"))
-        ta_sb.append(load_rows(ta, 2, "ta2"))
         w_sc_raw = load_scales(w_scales, "w_sc_raw")
+        tb_sb.append(load_rows(tb, 1, "tb1"))
+        xr_sc = load_scales(xr_scales, "xr_sc")
+        ta_sb.append(load_rows(ta, 2, "ta2"))
+        l5 = load_list(offs5, "l5")
+        ws_sc = load_scales(ws_scales, "ws_sc")
         tb_sb.append(load_rows(tb, 2, "tb2"))
+        wb_sc = load_scales(wb_scales, "wb_sc")
         sl_sb = load_factor(nc.sync, sl, "sl_sb")
+        w_raw = load_words(w_words[0], "w_raw")
         ta_sb.append(load_rows(ta, 3, "ta3"))
         l4 = load_list(offs4, "l4")
         tb_sb.append(load_rows(tb, 3, "tb3"))
-        w_raw = load_words(w_words[0], "w_raw")
+        base = sb.tile([P, PACK, J], F32, name="base")
+        sa_stage = base[:, PACK - 1, JH : JH + PACK]
+        nc.sync.dma_start(out=sa_stage, in_=sa.rearrange("(p t) o -> p (t o)", t=PACK))
+        sa_sb = sb.tile([P, PACK], F32, name="sa_sb")
+        nc.gpsimd.tensor_copy(out=sa_sb[:], in_=sa_stage)
         tl_sb = [load_rows(tl, 0, "tl0")]
         l3 = load_list(offs3, "l3")
-        sa_sb = load_factor(nc.sync, sa, "sa_sb")
         tl_sb.append(load_rows(tl, 1, "tl1"))
-        l5 = load_list(offs5, "l5")
-        xr_sc = load_scales(xr_scales, "xr_sc")
         tl_sb.append(load_rows(tl, 2, "tl2"))
-        ws_sc = load_scales(ws_scales, "ws_sc")
-        wb_sc = load_scales(wb_scales, "wb_sc")
         tl_sb.append(load_rows(tl, 3, "tl3"))
         xr_sb = load_words(xr_words[0].rearrange("p n t -> p (n t)"), "xr_sb")
         ws_sb = load_words(ws_words[0], "ws_sb")
@@ -127,98 +134,89 @@ def tile_picked_basedetail_plain_one_codedlevel_reminder_posted_kernel(
             in_=w_raw[:].rearrange("p (m t y) -> p t m y", t=PACK, y=2),
         )
 
-        base = sb.tile([P, PACK, J], F32, name="base")
         detail = sb.tile([P, PACK, J], F32, name="detail")
-        for t in range(PACK - 1):
+        xb = sb.tile([P, PACK * J], BF16, name="xb", align_bytes=64)
+        last = PACK - 1
+        for t in range(last):
             scaled_gather(base[:, t, :], ta_sb[t], l1[:], ga_sb[:, t : t + 1])
             scaled_gather(detail[:, t, :], tb_sb[t], l2[:], gb_sb[:, t : t + 1])
-        t = PACK - 1
-        scaled_gather(base[:, t, :], ta_sb[t], l1[:], ga_sb[:, t : t + 1])
-        a_sb = [sb.tile([P, J], F32, name="a%d" % t) for t in range(PACK)]
+        combine_pair(xb, base[:, 0:2, :], detail[:, 0:2, :], ADD, 0, J, 0)
         for h in range(HALVES):
             lo, hi = h * JH, (h + 1) * JH
-            scaled_gather(detail[:, PACK - 1, lo:hi], tb_sb[PACK - 1], cols16(l2, lo, hi), gb_sb[:, PACK - 1 : PACK])
-        banks1 = []
+            scaled_gather(base[:, last, lo:hi], ta_sb[last], cols16(l1, lo, hi), ga_sb[:, last : last + 1])
+            scaled_gather(detail[:, last, lo:hi], tb_sb[last], cols16(l2, lo, hi), gb_sb[:, last : last + 1])
+            combine_pair(xb, base[:, 2:4, :], detail[:, 2:4, :], ADD, lo, hi, 2)
+        xq = sb.tile([P, J], U32, name="xq", align_bytes=64)
+        xs = sb.tile([P, J], U8, name="xs", align_bytes=64)
+        a_ps = [ps.tile([P, J], F32, name="a_ps%d" % t) for t in range(PACK)]
         for h in range(HALVES):
             lo, hi = h * JH, (h + 1) * JH
-            xb = sb.tile([P, PACK * JH], BF16, name="xb%d" % h, align_bytes=64)
-            combine_interleaved(xb, base[:, :, lo:hi], detail[:, :, lo:hi], ADD)
-            xq = sb.tile([P, JH], U32, name="xq%d" % h, align_bytes=64)
-            xs = sb.tile([P, JH], U8, name="xs%d" % h, align_bytes=64)
-            nc.vector.quantize_mx(out=xq[:].bitcast(FP8X4), scales=xs[:], in_=xb[:])
-            pair = []
-            for u in range(2):
-                bank = ps.tile([P, 2, JH], F32, name="a_ps%d%d" % (h, u))
-                for v in range(2):
-                    t = 2 * u + v
-                    nc.tensor.matmul_mx(
-                        out=bank[:, v, :],
-                        lhsT=w_sb[:, 2 * P * t : 2 * P * (t + 1)].bitcast(FP4X4),
-                        lhsT_scale=w_sc[:, P * t : P * (t + 1)],
-                        rhs=xq[:].bitcast(FP8X4),
-                        rhs_scale=xs[:],
-                        start=True,
-                        stop=True,
-                    )
-                pair.append(bank)
-            banks1.append(pair)
+            nc.vector.quantize_mx(out=xq[:, lo:hi].bitcast(FP8X4), scales=xs[:, lo:hi], in_=xb[:, PACK * lo : PACK * hi])
+        for t in range(PACK):
+            for lo, hi in ((0, JH), (JH, J)) if t == 0 else ((0, J),):
+                nc.tensor.matmul_mx(
+                    out=a_ps[t][:, lo:hi],
+                    lhsT=w_sb[:, 2 * P * t : 2 * P * (t + 1)].bitcast(FP4X4),
+                    lhsT_scale=w_sc[:, P * t : P * (t + 1)],
+                    rhs=xq[:, lo:hi].bitcast(FP8X4),
+                    rhs_scale=xs[:, lo:hi],
+                    start=True,
+                    stop=True,
+                )
 
         level = sb.tile([P, PACK, O], F32, name="level")
-        for t in range(2):
+        for t in range(PACK):
             scaled_gather(level[:, t, :], tl_sb[t], l4[:], sl_sb[:, t : t + 1])
+        a_sb = [sb.tile([P, J], F32, name="a%d" % t) for t in range(PACK)]
         for t in range(PACK):
-            nc.scalar.copy(out=a_sb[t][:, 0:JH], in_=banks1[0][t // 2][:, t % 2, :])
-        for t in range(PACK):
-            nc.vector.tensor_copy(out=a_sb[t][:, JH:J], in_=banks1[1][t // 2][:, t % 2, :])
-        scaled_gather(level[:, 2, :], tl_sb[2], l4[:], sl_sb[:, 2:3])
+            nc.vector.tensor_copy(out=a_sb[t][:], in_=a_ps[t][:])
 
-        picked = sb.tile([P, PACK, O], F32, name="picked")
-        for t in range(PACK):
-            scaled_gather(picked[:, t, 0:OH], a_sb[t], cols16(l3, 0, OH), sa_sb[:, t : t + 1])
-        scaled_gather(level[:, 3, :], tl_sb[3], l4[:], sl_sb[:, 3:4])
-        for t in range(PACK):
-            scaled_gather(picked[:, t, OH:O], a_sb[t], cols16(l3, OH, O), sa_sb[:, t : t + 1])
+        picked = [sb.tile([P, 2, O], F32, name="picked%d" % u, tag="tl%d" % (2 + u)) for u in range(2)]
+        for t in range(last):
+            scaled_gather(picked[t // 2][:, t % 2, :], a_sb[t], l3[:], sa_sb[:, t : t + 1])
+        for h in range(HALVES):
+            lo, hi = h * OH, (h + 1) * OH
+            scaled_gather(picked[1][:, 1, lo:hi], a_sb[last], cols16(l3, lo, hi), sa_sb[:, last : last + 1])
 
         xr_gs = sb.tile([P, O], U8, name="xr_gs", align_bytes=64)
         nc.vector.tensor_copy(out=xr_gs[:], in_=xr_sc[:].indirect(l5[:]))
         xr_g = sb.tile([P, O], U32, name="xr_g", align_bytes=64)
-
-        p_sb = [sb.tile([P, O], F32, name="p%d" % b) for b in range(N // P)]
+        nc.vector.tensor_copy(out=xr_g[:], in_=xr_sb[:].bitcast(U32).indirect(l5[:]))
+        hb = sb.tile([P, PACK * O], BF16, name="hb", tag="xr_sb", align_bytes=64)
+        combine_pair(hb, picked[0], level[:, 0:2, :], MAX, 0, O, 0)
+        for h in range(HALVES):
+            combine_pair(hb, picked[1], level[:, 2:4, :], MAX, h * OH, (h + 1) * OH, 2)
+        hq = sb.tile([P, O], U32, name="hq", align_bytes=64)
+        hs = sb.tile([P, O], U8, name="hs", align_bytes=64)
         for h in range(HALVES):
             lo, hi = h * OH, (h + 1) * OH
-            hb = sb.tile([P, PACK * OH], BF16, name="hb%d" % h, align_bytes=64)
-            combine_interleaved(hb, picked[:, :, lo:hi], level[:, :, lo:hi], MAX)
-            hq = sb.tile([P, OH], U32, name="hq%d" % h, align_bytes=64)
-            hs = sb.tile([P, OH], U8, name="hs%d" % h, align_bytes=64)
-            nc.vector.quantize_mx(out=hq[:].bitcast(FP8X4), scales=hs[:], in_=hb[:])
-            if h == 0:
-                nc.vector.tensor_copy(out=xr_g[:], in_=xr_sb[:].bitcast(U32).indirect(l5[:]))
-            banks2 = []
-            for b in range(N // P):
-                bank = ps.tile([P, OH], F32, name="p_ps%d%d" % (h, b))
+            nc.vector.quantize_mx(out=hq[:, lo:hi].bitcast(FP8X4), scales=hs[:, lo:hi], in_=hb[:, PACK * lo : PACK * hi])
+        p_ps = [ps.tile([P, O], F32, name="p_ps%d" % b) for b in range(N // P)]
+        for b in range(N // P):
+            nc.tensor.matmul_mx(
+                out=p_ps[b][:],
+                lhsT=ws_sb[:, 2 * P * b : 2 * P * (b + 1)].bitcast(FP4X4),
+                lhsT_scale=ws_sc[:, P * b : P * (b + 1)],
+                rhs=xr_g[:].bitcast(FP8X4),
+                rhs_scale=xr_gs[:],
+                start=True,
+                stop=False,
+            )
+        for b in range(N // P):
+            for h in range(HALVES):
+                lo, hi = h * OH, (h + 1) * OH
                 nc.tensor.matmul_mx(
-                    out=bank[:],
-                    lhsT=ws_sb[:, 2 * P * b : 2 * P * (b + 1)].bitcast(FP4X4),
-                    lhsT_scale=ws_sc[:, P * b : P * (b + 1)],
-                    rhs=xr_g[:, lo:hi].bitcast(FP8X4),
-                    rhs_scale=xr_gs[:, lo:hi],
-                    start=True,
-                    stop=False,
-                )
-                banks2.append(bank)
-            for b in range(N // P):
-                nc.tensor.matmul_mx(
-                    out=banks2[b][:],
+                    out=p_ps[b][:, lo:hi],
                     lhsT=wb_sb[:, 4 * P * b : 4 * P * (b + 1)].bitcast(FP8X4),
                     lhsT_scale=wb_sc[:, P * b : P * (b + 1)],
-                    rhs=hq[:].bitcast(FP8X4),
-                    rhs_scale=hs[:],
+                    rhs=hq[:, lo:hi].bitcast(FP8X4),
+                    rhs_scale=hs[:, lo:hi],
                     start=False,
-                    stop=True,
+                    stop=(h == HALVES - 1),
                 )
-            for b in range(N // P):
-                nc.vector.tensor_copy(out=p_sb[b][:, lo:hi], in_=banks2[b][:])
-
+        p_sb = [sb.tile([P, O], F32, name="p%d" % b) for b in range(N // P)]
+        for b in range(N // P):
+            nc.vector.tensor_copy(out=p_sb[b][:], in_=p_ps[b][:])
         for b in range(N // P):
             ends = sb.tile([P, E], F32, name="ends%d" % b)
             scaled_gather(ends[:], p_sb[b], l6[:], so_sb[:, b : b + 1])

@@ -69,11 +69,12 @@ def tile_picked_basedetail_plain_one_codedlevel_reminder_posted_kernel(
         def scaled_gather(dst, window, offsets, factor):
             nc.scalar.activation(out=dst, in_=window[:].indirect(offsets), func=COPY, scale=factor)
 
-        def combine_pair(dst, left, right, op, lo, hi, t0):
+        def combine_planes(dst, left, right, op):
+            planes = left.shape[1]
             nc.vector.tensor_tensor(
-                out=dst[:, PACK * lo : PACK * hi].rearrange("p (c i t) -> p c t i", i=2, t=PACK)[:, :, t0 : t0 + 2, :],
-                in0=left[:, :, lo:hi].rearrange("p t (c i) -> p c t i", i=2),
-                in1=right[:, :, lo:hi].rearrange("p t (c i) -> p c t i", i=2),
+                out=dst.rearrange("p (c i t) -> p c t i", i=2, t=planes),
+                in0=left.rearrange("p t (c i) -> p c t i", i=2),
+                in1=right.rearrange("p t (c i) -> p c t i", i=2),
                 op=op,
             )
 
@@ -86,25 +87,34 @@ def tile_picked_basedetail_plain_one_codedlevel_reminder_posted_kernel(
         l1 = load_list(offs, "l1")
         l2 = load_list(offs2, "l2")
         tb_sb = [load_rows(tb, 0, "tb0")]
+        wb_sc = load_scales(wb_scales, "wb_sc")
+        xr_sc = sb.tile([P, Z], U8, name="xr_sc", align_bytes=64)
+        nc.vector.memset(xr_sc[:].bitcast(I32), 0)
+
+        def load_xr_scale_rows(i):
+            nc.sync.dma_start(out=xr_sc[i:P:32, :].bitcast(I32), in_=xr_scales[0].bitcast(I32)[i:16:4, :])
+
         ta_sb.append(load_rows(ta, 1, "ta1"))
-        w_sc_raw = load_scales(w_scales, "w_sc_raw")
+        load_xr_scale_rows(0)
+        load_xr_scale_rows(1)
         tb_sb.append(load_rows(tb, 1, "tb1"))
-        xr_sc = load_scales(xr_scales, "xr_sc")
+        load_xr_scale_rows(2)
+        load_xr_scale_rows(3)
         ta_sb.append(load_rows(ta, 2, "ta2"))
         l5 = load_list(offs5, "l5")
-        ws_sc = load_scales(ws_scales, "ws_sc")
+        w_sc_raw = load_scales(w_scales, "w_sc_raw")
         tb_sb.append(load_rows(tb, 2, "tb2"))
-        wb_sc = load_scales(wb_scales, "wb_sc")
-        sl_sb = load_factor(nc.sync, sl, "sl_sb")
+        ws_sc = load_scales(ws_scales, "ws_sc")
         w_raw = load_words(w_words[0], "w_raw")
         ta_sb.append(load_rows(ta, 3, "ta3"))
-        l4 = load_list(offs4, "l4")
         tb_sb.append(load_rows(tb, 3, "tb3"))
         base = sb.tile([P, PACK, J], F32, name="base")
         sa_stage = base[:, PACK - 1, JH : JH + PACK]
         nc.sync.dma_start(out=sa_stage, in_=sa.rearrange("(p t) o -> p (t o)", t=PACK))
         sa_sb = sb.tile([P, PACK], F32, name="sa_sb")
-        nc.gpsimd.tensor_copy(out=sa_sb[:], in_=sa_stage)
+        nc.scalar.copy(out=sa_sb[:], in_=sa_stage)
+        l4 = load_list(offs4, "l4")
+        sl_sb = load_factor(nc.sync, sl, "sl_sb")
         tl_sb = [load_rows(tl, 0, "tl0")]
         l3 = load_list(offs3, "l3")
         tl_sb.append(load_rows(tl, 1, "tl1"))
@@ -135,23 +145,31 @@ def tile_picked_basedetail_plain_one_codedlevel_reminder_posted_kernel(
         )
 
         detail = sb.tile([P, PACK, J], F32, name="detail")
-        xb = sb.tile([P, PACK * J], BF16, name="xb", align_bytes=64)
         last = PACK - 1
         for t in range(last):
             scaled_gather(base[:, t, :], ta_sb[t], l1[:], ga_sb[:, t : t + 1])
             scaled_gather(detail[:, t, :], tb_sb[t], l2[:], gb_sb[:, t : t + 1])
-        combine_pair(xb, base[:, 0:2, :], detail[:, 0:2, :], ADD, 0, J, 0)
+        pairs = [sb.tile([P, 2, 2 * JH], BF16, name="pairs%d" % h) for h in range(HALVES)]
+        for h in range(HALVES):
+            lo, hi = h * JH, (h + 1) * JH
+            combine_planes(pairs[h][:, 0, :], base[:, 0:2, lo:hi], detail[:, 0:2, lo:hi], ADD)
         for h in range(HALVES):
             lo, hi = h * JH, (h + 1) * JH
             scaled_gather(base[:, last, lo:hi], ta_sb[last], cols16(l1, lo, hi), ga_sb[:, last : last + 1])
             scaled_gather(detail[:, last, lo:hi], tb_sb[last], cols16(l2, lo, hi), gb_sb[:, last : last + 1])
-            combine_pair(xb, base[:, 2:4, :], detail[:, 2:4, :], ADD, lo, hi, 2)
+            combine_planes(pairs[h][:, 1, :], base[:, 2:4, lo:hi], detail[:, 2:4, lo:hi], ADD)
+        xb = [sb.tile([P, PACK * JH], BF16, name="xb%d" % h, align_bytes=64) for h in range(HALVES)]
+        for h in range(HALVES):
+            nc.vector.tensor_copy(
+                out=xb[h][:].bitcast(F32).rearrange("p (j u) -> p j u", u=2),
+                in_=pairs[h][:].bitcast(F32).rearrange("p u j -> p j u"),
+            )
         xq = sb.tile([P, J], U32, name="xq", align_bytes=64)
         xs = sb.tile([P, J], U8, name="xs", align_bytes=64)
         a_ps = [ps.tile([P, J], F32, name="a_ps%d" % t) for t in range(PACK)]
         for h in range(HALVES):
             lo, hi = h * JH, (h + 1) * JH
-            nc.vector.quantize_mx(out=xq[:, lo:hi].bitcast(FP8X4), scales=xs[:, lo:hi], in_=xb[:, PACK * lo : PACK * hi])
+            nc.vector.quantize_mx(out=xq[:, lo:hi].bitcast(FP8X4), scales=xs[:, lo:hi], in_=xb[h][:])
         for t in range(PACK):
             for lo, hi in ((0, JH), (JH, J)) if t == 0 else ((0, J),):
                 nc.tensor.matmul_mx(
@@ -171,21 +189,21 @@ def tile_picked_basedetail_plain_one_codedlevel_reminder_posted_kernel(
         for t in range(PACK):
             nc.vector.tensor_copy(out=a_sb[t][:], in_=a_ps[t][:])
 
-        picked = [sb.tile([P, 2, O], F32, name="picked%d" % u, tag="tl%d" % (2 + u)) for u in range(2)]
+        picked = sb.tile([P, PACK, O], F32, name="picked", tag="tl2")
         for t in range(last):
-            scaled_gather(picked[t // 2][:, t % 2, :], a_sb[t], l3[:], sa_sb[:, t : t + 1])
+            scaled_gather(picked[:, t, :], a_sb[t], l3[:], sa_sb[:, t : t + 1])
         for h in range(HALVES):
             lo, hi = h * OH, (h + 1) * OH
-            scaled_gather(picked[1][:, 1, lo:hi], a_sb[last], cols16(l3, lo, hi), sa_sb[:, last : last + 1])
+            scaled_gather(picked[:, last, lo:hi], a_sb[last], cols16(l3, lo, hi), sa_sb[:, last : last + 1])
 
         xr_gs = sb.tile([P, O], U8, name="xr_gs", align_bytes=64)
         nc.vector.tensor_copy(out=xr_gs[:], in_=xr_sc[:].indirect(l5[:]))
         xr_g = sb.tile([P, O], U32, name="xr_g", align_bytes=64)
         nc.vector.tensor_copy(out=xr_g[:], in_=xr_sb[:].bitcast(U32).indirect(l5[:]))
         hb = sb.tile([P, PACK * O], BF16, name="hb", tag="xr_sb", align_bytes=64)
-        combine_pair(hb, picked[0], level[:, 0:2, :], MAX, 0, O, 0)
         for h in range(HALVES):
-            combine_pair(hb, picked[1], level[:, 2:4, :], MAX, h * OH, (h + 1) * OH, 2)
+            lo, hi = h * OH, (h + 1) * OH
+            combine_planes(hb[:, PACK * lo : PACK * hi], picked[:, :, lo:hi], level[:, :, lo:hi], MAX)
         hq = sb.tile([P, O], U32, name="hq", align_bytes=64)
         hs = sb.tile([P, O], U8, name="hs", align_bytes=64)
         for h in range(HALVES):

from contextlib import ExitStack

import concourse.mybir as mybir

K, J, R, T, O, N, Z, E, G = 512, 512, 512, 1024, 256, 256, 1024, 128, 512
FLOPS = 2 * K * R * J + 2 * R * N * O + 2 * 512 * N * O

F32 = mybir.dt.float32
BF16 = mybir.dt.bfloat16
I32 = mybir.dt.int32
U32 = mybir.dt.uint32
U16 = mybir.dt.uint16
U8 = mybir.dt.uint8
FP8X4 = mybir.dt.float8_e4m3fn_x4
FP4X4 = mybir.dt.float4_e2m1fn_x4
COPY = mybir.ActivationFunctionType.Copy
ADD = mybir.AluOpType.add
MAX = mybir.AluOpType.max

P = 128
PACK = 4
HALVES = 2


def tile_picked_basedetail_plain_one_codedlevel_reminder_posted_kernel(
    tc, ta, tb, ga, gb, w_words, w_scales, tl, sa, sl, wb_words, wb_scales, xr_words, xr_scales,
    ws_words, ws_scales, so, offs, offs2, offs3, offs4, offs5, offs6, offs7, out,
):
    nc = tc.nc
    JH = J // HALVES
    OH = O // HALVES
    with ExitStack() as ctx:
        sb = ctx.enter_context(tc.tile_pool(name="sb", bufs=1))
        ps = ctx.enter_context(tc.psum_pool(name="ps", bufs=1))

        def load_list(src, name):
            dst = sb.tile(list(src.shape), U16, name=name)
            nc.sync.dma_start(dst[:], src)
            return dst

        def load_rows(table, t, name):
            dst = sb.tile([P, table.shape[1]], F32, name=name, tag=name)
            nc.sync.dma_start(out=dst[:], in_=table.rearrange("(p t) c -> p t c", t=PACK)[:, t, :])
            return dst

        def load_factor(engine, vec, name):
            dst = sb.tile([P, PACK], F32, name=name)
            engine.dma_start(out=dst[:], in_=vec.rearrange("(p t) o -> p (t o)", t=PACK))
            return dst

        def load_words(src, name):
            dst = sb.tile([P, src.shape[1]], U8, name=name, tag=name, align_bytes=64)
            nc.sync.dma_start(out=dst[:].bitcast(I32), in_=src.bitcast(I32))
            return dst

        def load_scales(src, name):
            width = src.shape[2]
            stage = sb.tile([4, 4, width // 4], I32, name=name + "_stage")
            nc.sync.dma_start(out=stage[:], in_=src[0].bitcast(I32).rearrange("(q i) c -> i q c", i=4))
            plane = sb.tile([P, width], U8, name=name, align_bytes=64)
            nc.vector.memset(plane[:].bitcast(I32), 0)
            for q in range(4):
                nc.vector.tensor_copy(out=plane[32 * q : 32 * q + 4, :].bitcast(I32), in_=stage[:, q, :])
            return plane

        def cols16(lst, lo, hi):
            return lst[:, lo // 16 : hi // 16]

        def scaled_gather(dst, window, offsets, factor):
            nc.scalar.activation(out=dst, in_=window[:].indirect(offsets), func=COPY, scale=factor)

        def combine_planes(dst, left, right, op):
            planes = left.shape[1]
            nc.vector.tensor_tensor(
                out=dst.rearrange("p (c i t) -> p c t i", i=2, t=planes),
                in0=left.rearrange("p t (c i) -> p c t i", i=2),
                in1=right.rearrange("p t (c i) -> p c t i", i=2),
                op=op,
            )

        warm = sb.tile([P, 2], F32, name="warm")
        nc.gpsimd.memset(warm[:, 0:1], 0.0)
        nc.scalar.activation(out=warm[:, 1:2], in_=warm[:, 0:1], func=COPY)
        ga_sb = load_factor(nc.scalar, ga, "ga_sb")
        gb_sb = load_factor(nc.scalar, gb, "gb_sb")
        ta_sb = [load_rows(ta, 0, "ta0")]
        l1 = load_list(offs, "l1")
        l2 = load_list(offs2, "l2")
        tb_sb = [load_rows(tb, 0, "tb0")]
        wb_sc = load_scales(wb_scales, "wb_sc")
        xr_sc = sb.tile([P, Z], U8, name="xr_sc", align_bytes=64)
        nc.vector.memset(xr_sc[:].bitcast(I32), 0)

        def load_xr_scale_rows(i):
            nc.sync.dma_start(out=xr_sc[i:P:32, :].bitcast(I32), in_=xr_scales[0].bitcast(I32)[i:16:4, :])

        ta_sb.append(load_rows(ta, 1, "ta1"))
        load_xr_scale_rows(0)
        load_xr_scale_rows(1)
        tb_sb.append(load_rows(tb, 1, "tb1"))
        load_xr_scale_rows(2)
        load_xr_scale_rows(3)
        ta_sb.append(load_rows(ta, 2, "ta2"))
        l5 = load_list(offs5, "l5")
        w_sc_raw = load_scales(w_scales, "w_sc_raw")
        tb_sb.append(load_rows(tb, 2, "tb2"))
        ws_sc = load_scales(ws_scales, "ws_sc")
        w_raw = load_words(w_words[0], "w_raw")
        ta_sb.append(load_rows(ta, 3, "ta3"))
        tb_sb.append(load_rows(tb, 3, "tb3"))
        base = sb.tile([P, PACK, J], F32, name="base")
        sa_stage = base[:, PACK - 1, JH : JH + PACK]
        nc.sync.dma_start(out=sa_stage, in_=sa.rearrange("(p t) o -> p (t o)", t=PACK))
        sa_sb = sb.tile([P, PACK], F32, name="sa_sb")
        nc.scalar.copy(out=sa_sb[:], in_=sa_stage)
        l4 = load_list(offs4, "l4")
        sl_sb = load_factor(nc.sync, sl, "sl_sb")
        tl_sb = [load_rows(tl, 0, "tl0")]
        l3 = load_list(offs3, "l3")
        tl_sb.append(load_rows(tl, 1, "tl1"))
        tl_sb.append(load_rows(tl, 2, "tl2"))
        tl_sb.append(load_rows(tl, 3, "tl3"))
        xr_sb = load_words(xr_words[0].rearrange("p n t -> p (n t)"), "xr_sb")
        ws_sb = load_words(ws_words[0], "ws_sb")
        wb_sb = load_words(wb_words[0].rearrange("p n t -> p (n t)"), "wb_sb")
        so_sb = sb.tile([P, N // P], F32, name="so_sb")
        with nc.allow_non_contiguous_dma(reason="one factor a partition"):
            nc.sync.dma_start(out=so_sb[:], in_=so.rearrange("(b p) o -> p (b o)", p=P))
        l6 = load_list(offs6, "l6")
        l7 = load_list(offs7, "l7")

        page = [sb.tile([P, G], F32, name="page%d" % b) for b in range(N // P)]
        for b in range(N // P):
            nc.vector.memset(page[b][:], 0.0)

        w_sc = sb.tile([P, R], U8, name="w_sc", align_bytes=64)
        nc.vector.tensor_copy(
            out=w_sc[:].rearrange("p (t m) -> p t m", t=PACK),
            in_=w_sc_raw[:].rearrange("p (m t) -> p t m", t=PACK),
        )
        w_sb = sb.tile([P, 2 * R], U8, name="w_sb", align_bytes=64)
        nc.vector.tensor_copy(
            out=w_sb[:].rearrange("p (t m y) -> p t m y", t=PACK, y=2),
            in_=w_raw[:].rearrange("p (m t y) -> p t m y", t=PACK, y=2),
        )

        detail = sb.tile([P, PACK, J], F32, name="detail")
        last = PACK - 1
        for t in range(last):
            scaled_gather(base[:, t, :], ta_sb[t], l1[:], ga_sb[:, t : t + 1])
            scaled_gather(detail[:, t, :], tb_sb[t], l2[:], gb_sb[:, t : t + 1])
        pairs = [sb.tile([P, 2, 2 * JH], BF16, name="pairs%d" % h) for h in range(HALVES)]
        for h in range(HALVES):
            lo, hi = h * JH, (h + 1) * JH
            combine_planes(pairs[h][:, 0, :], base[:, 0:2, lo:hi], detail[:, 0:2, lo:hi], ADD)
        for h in range(HALVES):
            lo, hi = h * JH, (h + 1) * JH
            scaled_gather(base[:, last, lo:hi], ta_sb[last], cols16(l1, lo, hi), ga_sb[:, last : last + 1])
            scaled_gather(detail[:, last, lo:hi], tb_sb[last], cols16(l2, lo, hi), gb_sb[:, last : last + 1])
            combine_planes(pairs[h][:, 1, :], base[:, 2:4, lo:hi], detail[:, 2:4, lo:hi], ADD)
        xb = [sb.tile([P, PACK * JH], BF16, name="xb%d" % h, align_bytes=64) for h in range(HALVES)]
        for h in range(HALVES):
            nc.vector.tensor_copy(
                out=xb[h][:].bitcast(F32).rearrange("p (j u) -> p j u", u=2),
                in_=pairs[h][:].bitcast(F32).rearrange("p u j -> p j u"),
            )
        xq = sb.tile([P, J], U32, name="xq", align_bytes=64)
        xs = sb.tile([P, J], U8, name="xs", align_bytes=64)
        a_ps = [ps.tile([P, J], F32, name="a_ps%d" % t) for t in range(PACK)]
        for h in range(HALVES):
            lo, hi = h * JH, (h + 1) * JH
            nc.vector.quantize_mx(out=xq[:, lo:hi].bitcast(FP8X4), scales=xs[:, lo:hi], in_=xb[h][:])
        for t in range(PACK):
            for lo, hi in ((0, JH), (JH, J)) if t == 0 else ((0, J),):
                nc.tensor.matmul_mx(
                    out=a_ps[t][:, lo:hi],
                    lhsT=w_sb[:, 2 * P * t : 2 * P * (t + 1)].bitcast(FP4X4),
                    lhsT_scale=w_sc[:, P * t : P * (t + 1)],
                    rhs=xq[:, lo:hi].bitcast(FP8X4),
                    rhs_scale=xs[:, lo:hi],
                    start=True,
                    stop=True,
                )

        level = sb.tile([P, PACK, O], F32, name="level")
        for t in range(PACK):
            scaled_gather(level[:, t, :], tl_sb[t], l4[:], sl_sb[:, t : t + 1])
        a_sb = [sb.tile([P, J], F32, name="a%d" % t) for t in range(PACK)]
        for t in range(PACK):
            nc.vector.tensor_copy(out=a_sb[t][:], in_=a_ps[t][:])

        picked = sb.tile([P, PACK, O], F32, name="picked", tag="tl2")
        for t in range(last):
            scaled_gather(picked[:, t, :], a_sb[t], l3[:], sa_sb[:, t : t + 1])
        for h in range(HALVES):
            lo, hi = h * OH, (h + 1) * OH
            scaled_gather(picked[:, last, lo:hi], a_sb[last], cols16(l3, lo, hi), sa_sb[:, last : last + 1])

        xr_gs = sb.tile([P, O], U8, name="xr_gs", align_bytes=64)
        nc.vector.tensor_copy(out=xr_gs[:], in_=xr_sc[:].indirect(l5[:]))
        xr_g = sb.tile([P, O], U32, name="xr_g", align_bytes=64)
        nc.vector.tensor_copy(out=xr_g[:], in_=xr_sb[:].bitcast(U32).indirect(l5[:]))
        hb = sb.tile([P, PACK * O], BF16, name="hb", tag="xr_sb", align_bytes=64)
        for h in range(HALVES):
            lo, hi = h * OH, (h + 1) * OH
            combine_planes(hb[:, PACK * lo : PACK * hi], picked[:, :, lo:hi], level[:, :, lo:hi], MAX)
        hq = sb.tile([P, O], U32, name="hq", align_bytes=64)
        hs = sb.tile([P, O], U8, name="hs", align_bytes=64)
        for h in range(HALVES):
            lo, hi = h * OH, (h + 1) * OH
            nc.vector.quantize_mx(out=hq[:, lo:hi].bitcast(FP8X4), scales=hs[:, lo:hi], in_=hb[:, PACK * lo : PACK * hi])
        p_ps = [ps.tile([P, O], F32, name="p_ps%d" % b) for b in range(N // P)]
        for b in range(N // P):
            nc.tensor.matmul_mx(
                out=p_ps[b][:],
                lhsT=ws_sb[:, 2 * P * b : 2 * P * (b + 1)].bitcast(FP4X4),
                lhsT_scale=ws_sc[:, P * b : P * (b + 1)],
                rhs=xr_g[:].bitcast(FP8X4),
                rhs_scale=xr_gs[:],
                start=True,
                stop=False,
            )
        for b in range(N // P):
            for h in range(HALVES):
                lo, hi = h * OH, (h + 1) * OH
                nc.tensor.matmul_mx(
                    out=p_ps[b][:, lo:hi],
                    lhsT=wb_sb[:, 4 * P * b : 4 * P * (b + 1)].bitcast(FP8X4),
                    lhsT_scale=wb_sc[:, P * b : P * (b + 1)],
                    rhs=hq[:, lo:hi].bitcast(FP8X4),
                    rhs_scale=hs[:, lo:hi],
                    start=False,
                    stop=(h == HALVES - 1),
                )
        p_sb = [sb.tile([P, O], F32, name="p%d" % b) for b in range(N // P)]
        for b in range(N // P):
            nc.vector.tensor_copy(out=p_sb[b][:], in_=p_ps[b][:])
        for b in range(N // P):
            ends = sb.tile([P, E], F32, name="ends%d" % b)
            scaled_gather(ends[:], p_sb[b], l6[:], so_sb[:, b : b + 1])
            nc.vector.tensor_copy(out=page[b][:].indirect(l7[:]), in_=ends[:])
            nc.sync.dma_start(out=out[P * b : P * (b + 1), :], in_=page[b][:])
